import numpy as np, ml_dtypes
CORES = [33,161,289,417,57,185,313,441]
N = 8
import mx_ref
NC, KT, ROOT = 256, 2, 0
BF = ml_dtypes.bfloat16
def cut(t, i, w=512):
    return t[:, w * i:w * i + w]
def pk(c, s, i=0):
    return (np.ascontiguousarray(c[:, 512 * i:512 * i + 512]), mx_ref.live(s[:, 128 * i:128 * i + 128]))
def inputs(rng, e, E):
    def f(*shape):
        v = (rng.standard_normal(shape, dtype=np.float32) * np.exp2(rng.integers(-2, 3, shape[:-1] + (1,)))).astype(BF)
        return mx_ref.spread((v.astype(np.float32) * np.exp2(rng.integers(-E, E + 1, shape[:-2] + (1, 1))).astype(np.float32)).astype(BF), rng, e)
    def packed(k):
        c = np.zeros((N, 128, k * 512), np.uint8); s = np.zeros((N, 128, k * 128), np.uint8)
        for r in range(N):
            for i in range(k):
                a, b = mx_ref.quantize(f(128, 512)); c[r][:, 512 * i:512 * i + 512] = a; s[r][:, 128 * i:128 * i + 128] = mx_ref.plane(b, rng)
        return c, s
    d = {}
    d["wc"], d["ws"] = packed(KT)
    d["x"] = f(N, 128, KT * 4 * NC)
    return d
def setup_inputs(rng):
    return inputs(rng, 0, 0)
def setup_inputs_blocks(rng):
    return inputs(rng, 4, 0)
def setup_inputs_wide(rng):
    return inputs(rng, 0, 8)
def reference(wc, ws, x):
    y = np.zeros((N, 128, NC), np.float32)
    for r in range(N):
        for t in range(KT):
            p = mx_ref.matmul(pk(wc[ROOT], ws[ROOT], t), mx_ref.quantize(cut(x[r], t, 4 * NC)))
            y[r] = p if t == 0 else y[r] + p
    return {"y": y}

@@ -1,0 +1,196 @@
+from concourse.bass import DstId, RemoteDMATransfer
+from concourse.mybir import dt
+
+KT = 2
+WCOL = 128
+XCOL = 256
+STAY = 4
+
+SCRATCH = {
+    "sd0": ("dram", [128, WCOL], "uint8"),
+    "sd1": ("dram", [128, WCOL], "uint8"),
+    "wd0": ("dram", [128, WCOL], "float8_e4m3fn_x4"),
+    "wd1": ("dram", [128, WCOL], "float8_e4m3fn_x4"),
+    "wq": ("sbuf", [128, KT * WCOL], "float8_e4m3fn_x4"),
+    "sq": ("sbuf", [128, KT * WCOL], "uint8"),
+    "xb": ("sbuf", [128, KT * 4 * XCOL], "bfloat16"),
+    "xq": ("sbuf", [128, KT * XCOL], "float8_e4m3fn_x4"),
+    "xs": ("sbuf", [128, KT * XCOL], "uint8"),
+    "ps": ("psum", [128, 512], "float32"),
+    "yo": ("sbuf", [128, XCOL], "float32"),
+}
+SEMAPHORES = ["ld_s", "ld_c", "go", "sent", "s_in", "c_in", "w0", "w1", "lx0", "lx1", "xq0", "xq1", "mm", "cp", "st"]
+
+
+def _bits(mask):
+    return [b for b in range(mask.bit_length()) if (mask >> b) & 1]
+
+
+def _mask(bits):
+    m = 0
+    for b in bits:
+        m |= 1 << b
+    return m
+
+
+def _same_chip(topo, a, b):
+    return topo.host(a) == topo.host(b) and topo.chip(a) == topo.chip(b)
+
+
+def _links(topo, a, b):
+    if _same_chip(topo, a, b):
+        return 0
+    if topo.rack(topo.host(a)) != topo.rack(topo.host(b)):
+        return 1 + _links(topo, a, b + (topo.host(a) - topo.host(b)) * topo.CORES_PER_HOST)
+    return 1 if (topo.mates(a, b) or topo.same_plane(a, b)) else 2
+
+
+def _share(bits, n):
+    k = 1
+    while 2 * k * n <= len(bits):
+        k *= 2
+    return [bits[i::n][:k] for i in range(n)]
+
+
+def _deal(topo, src, dsts):
+    off = [d for d in dsts if not _same_chip(topo, src, d)]
+    on = [d for d in dsts if _same_chip(topo, src, d)]
+    out, leave = {}, []
+    if off:
+        m = topo.mask(src, off[0])
+        for d in off:
+            m &= topo.mask(src, d)
+        leave = _bits(m)
+        for d, e in zip(off, _share(leave, len(off))):
+            out[d] = e
+    if on:
+        stay = [b for b in _bits(topo.mask(src, on[0])) if b not in leave][:STAY]
+        for d, e in zip(on, _share(stay, len(on))):
+            out[d] = e
+    return out
+
+
+def _plan(T, topo):
+    ranks = list(T.cores)
+    root = ranks[T.root]
+    world = range((1 + max(topo.host(c) for c in ranks)) * topo.CORES_PER_HOST)
+    gates = [root] + [d for d in ranks if d != root and topo.may_write(root, d)]
+    far = [d for d in ranks if not any(_same_chip(topo, d, gt) for gt in gates)]
+    dies = [topo.die(root)] + sorted(set(topo.die(c) for c in world if _same_chip(topo, c, root)) - {topo.die(root)})
+    spare = {gt: [c for c in world if _same_chip(topo, c, gt) and c not in ranks and topo.may_write(root, c)] for gt in gates}
+
+    def pick(gt, dests):
+        got = []
+        for die in dies[:KT]:
+            ok = [c for c in spare[gt] if topo.die(c) == die and all(topo.may_write(c, d) for d in dests)]
+            if not ok:
+                return None
+            got.append(ok[0])
+        return got
+
+    best = None
+    for code in range(len(gates) ** len(far)):
+        give = {gt: [] for gt in gates}
+        for i, d in enumerate(far):
+            give[gates[(code // len(gates) ** i) % len(gates)]].append(d)
+        if any(pick(gt, give[gt]) is None for gt in gates):
+            continue
+        cost = (max(len(v) for v in give.values()), sum(_links(topo, gt, d) for gt in gates for d in give[gt]),
+                sum(len(give[gt]) for gt in gates[1:]))
+        if best is None or cost < best[0]:
+            best = (cost, give)
+    give = best[1]
+    relays, feed = {}, []
+    picked = {gt: pick(gt, give[gt]) for gt in gates}
+    for t in range(KT):
+        for gt in gates:
+            relays[picked[gt][t]] = (t, ([] if gt == root else [gt]) + give[gt])
+            feed.append(picked[gt][t])
+    return root, relays, feed
+
+
+def _send(g, T, topo, core, deal, pieces, sem_name):
+    trs, n = [], 0
+    for d, src, dst in pieces:
+        rid, pid = topo.addr(d, core)
+        trs.append(RemoteDMATransfer(dst_ids=[DstId(rid=rid, pnc=pid)], dma_engine_mask=_mask(deal[d]),
+                                     remote_sem=T.sem[sem_name(d)], src=src, dst=dst))
+        n += len(deal[d])
+    g.remote_dma_fused(trs, local_sem=T.sem.sent)
+    return n
+
+
+def _plane_d(T, t):
+    return T["sd%d" % t][:]
+
+
+def _codes_d(T, t):
+    return T["wd%d" % t][:].bitcast(dt.uint8)
+
+
+def rank_program(g, core, T, topo):
+    root, relays, feed = _plan(T, topo)
+    sem = T.sem
+
+    if core in relays:
+        t, dests = relays[core]
+        got = len(_deal(topo, root, feed)[core])
+        deal = _deal(topo, core, dests)
+        a, b = t * WCOL, (t + 1) * WCOL
+        g.wait_ge(sem.s_in, got)
+        n = _send(g, T, topo, core, deal, [(d, _plane_d(T, t), T.sq[:, a:b]) for d in dests], lambda d: "w%d" % t)
+        g.wait_ge(sem.c_in, got)
+        n += _send(g, T, topo, core, deal, [(d, _codes_d(T, t), T.wq[:, a:b].bitcast(dt.uint8)) for d in dests],
+                   lambda d: "w%d" % t)
+        g.wait_ge(sem.sent, n)
+        return
+
+    if T.rank_of(core) is None:
+        return
+
+    queues = [g.sync, g.scalar]
+    if core == root:
+        for t in range(KT):
+            queues[t].dma_start(_plane_d(T, t), T.ws[:, t * WCOL:(t + 1) * WCOL]).then_inc(sem.ld_s, 16)
+        for t in range(KT):
+            queues[t].dma_start(_codes_d(T, t), T.wc[:, 4 * t * WCOL:4 * (t + 1) * WCOL]).then_inc(sem.ld_c, 16)
+        g.sync.dma_start(T.wq[:].bitcast(dt.uint8), T.wc[:, :]).then_inc(sem.w0, 16)
+        g.scalar.dma_start(T.sq[:], T.ws[:, :]).then_inc(sem.w0, 16)
+        need = [32, 0]
+        deal = _deal(topo, root, feed)
+        g.wait_ge(sem.ld_s, 16 * KT)
+        n = _send(g, T, topo, core, deal, [(r, _plane_d(T, relays[r][0]), _plane_d(T, relays[r][0])) for r in feed],
+                  lambda d: "s_in")
+        g.wait_ge(sem.ld_c, 16 * KT)
+        n += _send(g, T, topo, core, deal, [(r, _codes_d(T, relays[r][0]), _codes_d(T, relays[r][0])) for r in feed],
+                   lambda d: "c_in")
+        g.sem_inc(sem.go, 1)
+        for q in queues:
+            q.wait_ge(sem.go, 1)
+    else:
+        need = [0] * KT
+        for r, (t, dests) in relays.items():
+            if core in dests:
+                need[t] = 2 * len(_deal(topo, r, dests)[core])
+
+    for t in range(KT):
+        queues[t].dma_start(T.xb[:, 4 * t * XCOL:4 * (t + 1) * XCOL], T.x[:, 4 * t * XCOL:4 * (t + 1) * XCOL]).then_inc(
+            sem["lx%d" % t], 16)
+    for t in range(KT):
+        g.vector.wait_ge(sem["lx%d" % t], 16)
+        g.vector.quantize_mx(T.xq[:, t * XCOL:(t + 1) * XCOL], T.xs[:, t * XCOL:(t + 1) * XCOL],
+                             T.xb[:, 4 * t * XCOL:4 * (t + 1) * XCOL]).then_inc(sem["xq%d" % t], 1)
+    for t in range(KT):
+        if need[t]:
+            g.tensor.wait_ge(sem["w%d" % t], need[t])
+        g.tensor.wait_ge(sem["xq%d" % t], 1)
+        mm = g.tensor.matmul_mx(T.ps[:, 0:XCOL], T.wq[:, t * WCOL:(t + 1) * WCOL], T.sq[:, t * WCOL:(t + 1) * WCOL],
+                                T.xq[:, t * XCOL:(t + 1) * XCOL], T.xs[:, t * XCOL:(t + 1) * XCOL], t == 0, t == KT - 1)
+    mm.then_inc(sem.mm, 1)
+    g.vector.wait_ge(sem.mm, 1)
+    g.vector.tensor_copy(T.yo[:], T.ps[:, 0:XCOL]).then_inc(sem.cp, 1)
+    g.sync.wait_ge(sem.cp, 1)
+    g.sync.dma_start(T.y[:, :], T.yo[:]).then_inc(sem.st, 16)
+    g.sync.wait_ge(sem.st, 16)
+    if core == root:
+        g.wait_ge(sem.sent, n)

@@ -4,22 +4,28 @@ from concourse.mybir import dt
 KT = 2
 WCOL = 128
 XCOL = 256
-STAY = 4
+HCOL = 128
+PER = 2
+NCH = 2
+CCOL = WCOL // NCH
 
 SCRATCH = {
     "sd0": ("dram", [128, WCOL], "uint8"),
     "sd1": ("dram", [128, WCOL], "uint8"),
-    "wd0": ("dram", [128, WCOL], "float8_e4m3fn_x4"),
-    "wd1": ("dram", [128, WCOL], "float8_e4m3fn_x4"),
     "wq": ("sbuf", [128, KT * WCOL], "float8_e4m3fn_x4"),
     "sq": ("sbuf", [128, KT * WCOL], "uint8"),
     "xb": ("sbuf", [128, KT * 4 * XCOL], "bfloat16"),
     "xq": ("sbuf", [128, KT * XCOL], "float8_e4m3fn_x4"),
     "xs": ("sbuf", [128, KT * XCOL], "uint8"),
-    "ps": ("psum", [128, 512], "float32"),
+    "ps": ("psum", [128, 1024], "float32"),
     "yo": ("sbuf", [128, XCOL], "float32"),
 }
-SEMAPHORES = ["ld_s", "ld_c", "go", "sent", "s_in", "c_in", "w0", "w1", "lx0", "lx1", "xq0", "xq1", "mm", "cp", "st"]
+for _t in range(KT):
+    for _k in range(NCH):
+        SCRATCH["wd%d_%d" % (_t, _k)] = ("dram", [128, CCOL], "float8_e4m3fn_x4")
+SEMAPHORES = ["ld_s", "sent", "s_in", "p0", "p1", "q0", "q1", "w0", "w1",
+              "lx0", "lx1", "xq0", "xq1", "mm0", "mm1", "cp0", "cp1", "st0", "st1"]
+SEMAPHORES += ["lc%d" % _k for _k in range(NCH)] + ["ci%d" % _k for _k in range(NCH)]
 
 
 def _bits(mask):
@@ -55,57 +61,62 @@ def _share(bits, n):
 def _deal(topo, src, dsts):
     off = [d for d in dsts if not _same_chip(topo, src, d)]
     on = [d for d in dsts if _same_chip(topo, src, d)]
-    out, leave = {}, []
-    if off:
-        m = topo.mask(src, off[0])
-        for d in off:
-            m &= topo.mask(src, d)
-        leave = _bits(m)
-        for d, e in zip(off, _share(leave, len(off))):
-            out[d] = e
+    m = topo.mask(src, off[0])
+    for d in off:
+        m &= topo.mask(src, d)
+    leave = _bits(m)
+    out = dict(zip(off, _share(leave, len(off))))
     if on:
-        stay = [b for b in _bits(topo.mask(src, on[0])) if b not in leave][:STAY]
-        for d, e in zip(on, _share(stay, len(on))):
-            out[d] = e
+        stay = [b for b in _bits(topo.mask(src, on[0])) if b not in leave]
+        out.update(zip(on, _share(stay, len(on))))
     return out
+
+
+def _first(deal):
+    return {d: e[:1] for d, e in deal.items()}
+
+
+def _perms(items):
+    if not items:
+        return [[]]
+    return [[x] + p for i, x in enumerate(items) for p in _perms(items[:i] + items[i + 1:])]
 
 
 def _plan(T, topo):
     ranks = list(T.cores)
     root = ranks[T.root]
     world = range((1 + max(topo.host(c) for c in ranks)) * topo.CORES_PER_HOST)
-    gates = [root] + [d for d in ranks if d != root and topo.may_write(root, d)]
-    far = [d for d in ranks if not any(_same_chip(topo, d, gt) for gt in gates)]
     dies = [topo.die(root)] + sorted(set(topo.die(c) for c in world if _same_chip(topo, c, root)) - {topo.die(root)})
-    spare = {gt: [c for c in world if _same_chip(topo, c, gt) and c not in ranks and topo.may_write(root, c)] for gt in gates}
 
-    def pick(gt, dests):
-        got = []
-        for die in dies[:KT]:
-            ok = [c for c in spare[gt] if topo.die(c) == die and all(topo.may_write(c, d) for d in dests)]
-            if not ok:
-                return None
-            got.append(ok[0])
-        return got
+    def spare(chip_of):
+        return [c for c in world if _same_chip(topo, c, chip_of) and c not in ranks and topo.may_write(root, c)]
+
+    def pick(chip_of, t, dests, used):
+        ok = [c for c in spare(chip_of) if topo.die(c) == dies[t] and c not in used and all(topo.may_write(c, d) for d in dests)]
+        return ok[0] if ok else None
+
+    gates = [d for d in ranks if d != root and topo.may_write(root, d)]
+    far = [d for d in ranks if d != root and d not in gates]
+    away = [d for d in far if not any(topo.may_write(c, d) for c in spare(root))]
+    near = sorted((d for d in far if d not in away), key=lambda d: _links(topo, root, d))
 
     best = None
-    for code in range(len(gates) ** len(far)):
-        give = {gt: [] for gt in gates}
-        for i, d in enumerate(far):
-            give[gates[(code // len(gates) ** i) % len(gates)]].append(d)
-        if any(pick(gt, give[gt]) is None for gt in gates):
+    for p in _perms(gates):
+        pairs = list(zip(p, away))
+        if any(pick(gt, t, [d], []) is None for gt, d in pairs for t in range(KT)):
             continue
-        cost = (max(len(v) for v in give.values()), sum(_links(topo, gt, d) for gt in gates for d in give[gt]),
-                sum(len(give[gt]) for gt in gates[1:]))
+        cost = sum(_links(topo, gt, d) for gt, d in pairs)
         if best is None or cost < best[0]:
-            best = (cost, give)
-    give = best[1]
+            best = (cost, dict(pairs))
+    groups = [(gt, [gt] + ([best[1][gt]] if gt in best[1] else [])) for gt in gates]
+    groups += [(root, near[i:i + PER]) for i in range(0, len(near), PER)]
+
     relays, feed = {}, []
-    picked = {gt: pick(gt, give[gt]) for gt in gates}
     for t in range(KT):
-        for gt in gates:
-            relays[picked[gt][t]] = (t, ([] if gt == root else [gt]) + give[gt])
-            feed.append(picked[gt][t])
+        for chip_of, dests in groups:
+            r = pick(chip_of, t, [d for d in dests if not _same_chip(topo, d, chip_of)], relays)
+            relays[r] = (t, dests)
+            feed.append(r)
     return root, relays, feed
 
 
@@ -114,7 +125,7 @@ def _send(g, T, topo, core, deal, pieces, sem_name):
     for d, src, dst in pieces:
         rid, pid = topo.addr(d, core)
         trs.append(RemoteDMATransfer(dst_ids=[DstId(rid=rid, pnc=pid)], dma_engine_mask=_mask(deal[d]),
-                                     remote_sem=T.sem[sem_name(d)], src=src, dst=dst))
+                                     remote_sem=T.sem[sem_name], src=src, dst=dst))
         n += len(deal[d])
     g.remote_dma_fused(trs, local_sem=T.sem.sent)
     return n
@@ -124,8 +135,14 @@ def _plane_d(T, t):
     return T["sd%d" % t][:]
 
 
-def _codes_d(T, t):
-    return T["wd%d" % t][:].bitcast(dt.uint8)
+def _codes_d(T, t, k):
+    return T["wd%d_%d" % (t, k)][:].bitcast(dt.uint8)
+
+
+def _load_x(T, queues):
+    for t in range(KT):
+        queues[t].dma_start(T.xb[:, 4 * t * XCOL:4 * (t + 1) * XCOL], T.x[:, 4 * t * XCOL:4 * (t + 1) * XCOL]).then_inc(
+            T.sem["lx%d" % t], 16)
 
 
 def rank_program(g, core, T, topo):
@@ -134,14 +151,15 @@ def rank_program(g, core, T, topo):
 
     if core in relays:
         t, dests = relays[core]
-        got = len(_deal(topo, root, feed)[core])
+        fed = _deal(topo, root, feed)
         deal = _deal(topo, core, dests)
-        a, b = t * WCOL, (t + 1) * WCOL
-        g.wait_ge(sem.s_in, got)
-        n = _send(g, T, topo, core, deal, [(d, _plane_d(T, t), T.sq[:, a:b]) for d in dests], lambda d: "w%d" % t)
-        g.wait_ge(sem.c_in, got)
-        n += _send(g, T, topo, core, deal, [(d, _codes_d(T, t), T.wq[:, a:b].bitcast(dt.uint8)) for d in dests],
-                   lambda d: "w%d" % t)
+        g.wait_ge(sem.s_in, len(_first(fed)[core]))
+        n = _send(g, T, topo, core, deal, [(d, _plane_d(T, t), _plane_d(T, t)) for d in dests], "p%d" % t)
+        for k in range(NCH):
+            a = t * WCOL + k * CCOL
+            g.wait_ge(sem["ci%d" % k], len(fed[core]))
+            n += _send(g, T, topo, core, deal, [(d, _codes_d(T, t, k), T.wq[:, a:a + CCOL].bitcast(dt.uint8)) for d in dests],
+                       "w%d" % t)
         g.wait_ge(sem.sent, n)
         return
 
@@ -152,45 +170,54 @@ def rank_program(g, core, T, topo):
     if core == root:
         for t in range(KT):
             queues[t].dma_start(_plane_d(T, t), T.ws[:, t * WCOL:(t + 1) * WCOL]).then_inc(sem.ld_s, 16)
-        for t in range(KT):
-            queues[t].dma_start(_codes_d(T, t), T.wc[:, 4 * t * WCOL:4 * (t + 1) * WCOL]).then_inc(sem.ld_c, 16)
+        for k in range(NCH):
+            for t in range(KT):
+                a = 4 * (t * WCOL + k * CCOL)
+                queues[t].dma_start(_codes_d(T, t, k), T.wc[:, a:a + 4 * CCOL]).then_inc(sem["lc%d" % k], 16)
+        _load_x(T, queues)
         g.sync.dma_start(T.wq[:].bitcast(dt.uint8), T.wc[:, :]).then_inc(sem.w0, 16)
         g.scalar.dma_start(T.sq[:], T.ws[:, :]).then_inc(sem.w0, 16)
-        need = [32, 0]
         deal = _deal(topo, root, feed)
         g.wait_ge(sem.ld_s, 16 * KT)
-        n = _send(g, T, topo, core, deal, [(r, _plane_d(T, relays[r][0]), _plane_d(T, relays[r][0])) for r in feed],
-                  lambda d: "s_in")
-        g.wait_ge(sem.ld_c, 16 * KT)
-        n += _send(g, T, topo, core, deal, [(r, _codes_d(T, relays[r][0]), _codes_d(T, relays[r][0])) for r in feed],
-                   lambda d: "c_in")
-        g.sem_inc(sem.go, 1)
-        for q in queues:
-            q.wait_ge(sem.go, 1)
+        n = _send(g, T, topo, core, _first(deal), [(r, _plane_d(T, relays[r][0]), _plane_d(T, relays[r][0])) for r in feed], "s_in")
+        for k in range(NCH):
+            g.wait_ge(sem["lc%d" % k], 16 * KT)
+            n += _send(g, T, topo, core, deal, [(r, _codes_d(T, relays[r][0], k), _codes_d(T, relays[r][0], k)) for r in feed],
+                       "ci%d" % k)
     else:
-        need = [0] * KT
+        lanes = [0] * KT
         for r, (t, dests) in relays.items():
             if core in dests:
-                need[t] = 2 * len(_deal(topo, r, dests)[core])
+                lanes[t] = len(_deal(topo, r, dests)[core])
+        _load_x(T, queues)
+        for t in range(KT):
+            queues[t].wait_ge(sem["p%d" % t], lanes[t])
+            queues[t].dma_start(T.sq[:, t * WCOL:(t + 1) * WCOL], _plane_d(T, t)).then_inc(sem["q%d" % t], 16)
 
-    for t in range(KT):
-        queues[t].dma_start(T.xb[:, 4 * t * XCOL:4 * (t + 1) * XCOL], T.x[:, 4 * t * XCOL:4 * (t + 1) * XCOL]).then_inc(
-            sem["lx%d" % t], 16)
     for t in range(KT):
         g.vector.wait_ge(sem["lx%d" % t], 16)
         g.vector.quantize_mx(T.xq[:, t * XCOL:(t + 1) * XCOL], T.xs[:, t * XCOL:(t + 1) * XCOL],
                              T.xb[:, 4 * t * XCOL:4 * (t + 1) * XCOL]).then_inc(sem["xq%d" % t], 1)
-    for t in range(KT):
-        if need[t]:
-            g.tensor.wait_ge(sem["w%d" % t], need[t])
-        g.tensor.wait_ge(sem["xq%d" % t], 1)
-        mm = g.tensor.matmul_mx(T.ps[:, 0:XCOL], T.wq[:, t * WCOL:(t + 1) * WCOL], T.sq[:, t * WCOL:(t + 1) * WCOL],
-                                T.xq[:, t * XCOL:(t + 1) * XCOL], T.xs[:, t * XCOL:(t + 1) * XCOL], t == 0, t == KT - 1)
-    mm.then_inc(sem.mm, 1)
-    g.vector.wait_ge(sem.mm, 1)
-    g.vector.tensor_copy(T.yo[:], T.ps[:, 0:XCOL]).then_inc(sem.cp, 1)
-    g.sync.wait_ge(sem.cp, 1)
-    g.sync.dma_start(T.y[:, :], T.yo[:]).then_inc(sem.st, 16)
-    g.sync.wait_ge(sem.st, 16)
+    for h in range(2):
+        for t in range(KT):
+            if h == 0:
+                if core == root:
+                    if t == 0:
+                        g.tensor.wait_ge(sem.w0, 32)
+                else:
+                    g.tensor.wait_ge(sem["q%d" % t], 16)
+                    g.tensor.wait_ge(sem["w%d" % t], NCH * lanes[t])
+                g.tensor.wait_ge(sem["xq%d" % t], 1)
+            c = t * XCOL + h * HCOL
+            mm = g.tensor.matmul_mx(T.ps[:, 512 * h:512 * h + HCOL], T.wq[:, t * WCOL:(t + 1) * WCOL],
+                                    T.sq[:, t * WCOL:(t + 1) * WCOL], T.xq[:, c:c + HCOL], T.xs[:, c:c + HCOL], t == 0, t == KT - 1)
+        mm.then_inc(sem["mm%d" % h], 1)
+    for h in range(2):
+        g.vector.wait_ge(sem["mm%d" % h], 1)
+        g.vector.tensor_copy(T.yo[:, h * HCOL:(h + 1) * HCOL], T.ps[:, 512 * h:512 * h + HCOL]).then_inc(sem["cp%d" % h], 1)
+    for h in range(2):
+        queues[h].wait_ge(sem["cp%d" % h], 1)
+        queues[h].dma_start(T.y[:, h * HCOL:(h + 1) * HCOL], T.yo[:, h * HCOL:(h + 1) * HCOL]).then_inc(sem["st%d" % h], 16)
+        queues[h].wait_ge(sem["st%d" % h], 16)
     if core == root:
         g.wait_ge(sem.sent, n)

@@ -61,11 +61,13 @@ def _share(bits, n):
 def _deal(topo, src, dsts):
     off = [d for d in dsts if not _same_chip(topo, src, d)]
     on = [d for d in dsts if _same_chip(topo, src, d)]
-    m = topo.mask(src, off[0])
-    for d in off:
-        m &= topo.mask(src, d)
-    leave = _bits(m)
-    out = dict(zip(off, _share(leave, len(off))))
+    leave, out = [], {}
+    if off:
+        m = topo.mask(src, off[0])
+        for d in off:
+            m &= topo.mask(src, d)
+        leave = _bits(m)
+        out.update(zip(off, _share(leave, len(off))))
     if on:
         stay = [b for b in _bits(topo.mask(src, on[0])) if b not in leave]
         out.update(zip(on, _share(stay, len(on))))
@@ -76,48 +78,45 @@ def _first(deal):
     return {d: e[:1] for d, e in deal.items()}
 
 
-def _perms(items):
-    if not items:
-        return [[]]
-    return [[x] + p for i, x in enumerate(items) for p in _perms(items[:i] + items[i + 1:])]
-
-
 def _plan(T, topo):
     ranks = list(T.cores)
     root = ranks[T.root]
     world = range((1 + max(topo.host(c) for c in ranks)) * topo.CORES_PER_HOST)
     dies = [topo.die(root)] + sorted(set(topo.die(c) for c in world if _same_chip(topo, c, root)) - {topo.die(root)})
 
+    def rack(c):
+        return topo.rack(topo.host(c))
+
     def spare(chip_of):
         return [c for c in world if _same_chip(topo, c, chip_of) and c not in ranks and topo.may_write(root, c)]
 
     def pick(chip_of, t, dests, used):
         ok = [c for c in spare(chip_of) if topo.die(c) == dies[t] and c not in used and all(topo.may_write(c, d) for d in dests)]
-        return ok[0] if ok else None
+        return min(ok, key=lambda c: sum(topo.may_write(c, d) for d in ranks))
 
-    gates = [d for d in ranks if d != root and topo.may_write(root, d)]
-    far = [d for d in ranks if d != root and d not in gates]
-    away = [d for d in far if not any(topo.may_write(c, d) for c in spare(root))]
-    near = sorted((d for d in far if d not in away), key=lambda d: _links(topo, root, d))
+    bases = [root] + [d for d in ranks if d != root and topo.may_write(root, d) and rack(d) == rack(root)]
+    served = dict((b, []) for b in bases)
+    for d in ranks:
+        if d != root:
+            ok = [b for b in bases if any(topo.may_write(c, d) for c in spare(b))]
+            served[min(ok, key=lambda b: _links(topo, b, d))].append(d)
+    groups = []
+    for b in bases:
+        far = sorted((d for d in served[b] if rack(d) != rack(b)), key=lambda d: _links(topo, b, d))
+        own = [d for d in served[b] if _same_chip(topo, d, b)]
+        rest = [d for d in served[b] if d not in far and d not in own]
+        gs = [[d] for d in far] + [rest[i:i + PER] for i in range(0, len(rest), PER)]
+        gs[0] = gs[0] + own
+        groups += [(b, ds) for ds in gs]
 
-    best = None
-    for p in _perms(gates):
-        pairs = list(zip(p, away))
-        if any(pick(gt, t, [d], []) is None for gt, d in pairs for t in range(KT)):
-            continue
-        cost = sum(_links(topo, gt, d) for gt, d in pairs)
-        if best is None or cost < best[0]:
-            best = (cost, dict(pairs))
-    groups = [(gt, [gt] + ([best[1][gt]] if gt in best[1] else [])) for gt in gates]
-    groups += [(root, near[i:i + PER]) for i in range(0, len(near), PER)]
-
-    relays, feed = {}, []
+    relays, waves = {}, [[], []]
     for t in range(KT):
-        for chip_of, dests in groups:
-            r = pick(chip_of, t, [d for d in dests if not _same_chip(topo, d, chip_of)], relays)
+        for b, dests in groups:
+            r = pick(b, t, [d for d in dests if not _same_chip(topo, d, b)], relays)
             relays[r] = (t, dests)
-            feed.append(r)
-    return root, relays, feed
+            first = not _same_chip(topo, r, root) or any(rack(d) != rack(r) for d in dests)
+            waves[0 if first else 1].append(r)
+    return root, relays, [w for w in waves if w]
 
 
 def _send(g, T, topo, core, deal, pieces, sem_name):
@@ -146,14 +145,16 @@ def _load_x(T, queues):
 
 
 def rank_program(g, core, T, topo):
-    root, relays, feed = _plan(T, topo)
+    root, relays, waves = _plan(T, topo)
     sem = T.sem
+    fed_p = _first(_deal(topo, root, [r for w in waves for r in w]))
+    fed_c = [_deal(topo, root, w) for w in waves]
 
     if core in relays:
         t, dests = relays[core]
-        fed = _deal(topo, root, feed)
+        fed = [f for f in fed_c if core in f][0]
         deal = _deal(topo, core, dests)
-        g.wait_ge(sem.s_in, len(_first(fed)[core]))
+        g.wait_ge(sem.s_in, len(fed_p[core]))
         n = _send(g, T, topo, core, deal, [(d, _plane_d(T, t), _plane_d(T, t)) for d in dests], "p%d" % t)
         for k in range(NCH):
             a = t * WCOL + k * CCOL
@@ -177,13 +178,13 @@ def rank_program(g, core, T, topo):
         _load_x(T, queues)
         g.sync.dma_start(T.wq[:].bitcast(dt.uint8), T.wc[:, :]).then_inc(sem.w0, 16)
         g.scalar.dma_start(T.sq[:], T.ws[:, :]).then_inc(sem.w0, 16)
-        deal = _deal(topo, root, feed)
         g.wait_ge(sem.ld_s, 16 * KT)
-        n = _send(g, T, topo, core, _first(deal), [(r, _plane_d(T, relays[r][0]), _plane_d(T, relays[r][0])) for r in feed], "s_in")
+        n = _send(g, T, topo, core, fed_p, [(r, _plane_d(T, relays[r][0]), _plane_d(T, relays[r][0])) for r in fed_p], "s_in")
         for k in range(NCH):
             g.wait_ge(sem["lc%d" % k], 16 * KT)
-            n += _send(g, T, topo, core, deal, [(r, _codes_d(T, relays[r][0], k), _codes_d(T, relays[r][0], k)) for r in feed],
-                       "ci%d" % k)
+            for w, f in zip(waves, fed_c):
+                n += _send(g, T, topo, core, f, [(r, _codes_d(T, relays[r][0], k), _codes_d(T, relays[r][0], k)) for r in w],
+                           "ci%d" % k)
     else:
         lanes = [0] * KT
         for r, (t, dests) in relays.items():

from concourse.bass import DstId, RemoteDMATransfer
from concourse.mybir import dt

KT = 2
WCOL = 128
XCOL = 256
HCOL = 128
PER = 2
NCH = 2
CCOL = WCOL // NCH

SCRATCH = {
    "sd0": ("dram", [128, WCOL], "uint8"),
    "sd1": ("dram", [128, WCOL], "uint8"),
    "wq": ("sbuf", [128, KT * WCOL], "float8_e4m3fn_x4"),
    "sq": ("sbuf", [128, KT * WCOL], "uint8"),
    "xb": ("sbuf", [128, KT * 4 * XCOL], "bfloat16"),
    "xq": ("sbuf", [128, KT * XCOL], "float8_e4m3fn_x4"),
    "xs": ("sbuf", [128, KT * XCOL], "uint8"),
    "ps": ("psum", [128, 1024], "float32"),
    "yo": ("sbuf", [128, XCOL], "float32"),
}
for _t in range(KT):
    for _k in range(NCH):
        SCRATCH["wd%d_%d" % (_t, _k)] = ("dram", [128, CCOL], "float8_e4m3fn_x4")
SEMAPHORES = ["ld_s", "sent", "s_in", "p0", "p1", "q0", "q1", "w0", "w1",
              "lx0", "lx1", "xq0", "xq1", "mm0", "mm1", "cp0", "cp1", "st0", "st1"]
SEMAPHORES += ["lc%d" % _k for _k in range(NCH)] + ["ci%d" % _k for _k in range(NCH)]


def _bits(mask):
    return [b for b in range(mask.bit_length()) if (mask >> b) & 1]


def _mask(bits):
    m = 0
    for b in bits:
        m |= 1 << b
    return m


def _same_chip(topo, a, b):
    return topo.host(a) == topo.host(b) and topo.chip(a) == topo.chip(b)


def _links(topo, a, b):
    if _same_chip(topo, a, b):
        return 0
    if topo.rack(topo.host(a)) != topo.rack(topo.host(b)):
        return 1 + _links(topo, a, b + (topo.host(a) - topo.host(b)) * topo.CORES_PER_HOST)
    return 1 if (topo.mates(a, b) or topo.same_plane(a, b)) else 2


def _share(bits, n):
    k = 1
    while 2 * k * n <= len(bits):
        k *= 2
    return [bits[i::n][:k] for i in range(n)]


def _deal(topo, src, dsts):
    off = [d for d in dsts if not _same_chip(topo, src, d)]
    on = [d for d in dsts if _same_chip(topo, src, d)]
    leave, out = [], {}
    if off:
        m = topo.mask(src, off[0])
        for d in off:
            m &= topo.mask(src, d)
        leave = _bits(m)
        out.update(zip(off, _share(leave, len(off))))
    if on:
        stay = [b for b in _bits(topo.mask(src, on[0])) if b not in leave]
        out.update(zip(on, _share(stay, len(on))))
    return out


def _first(deal):
    return {d: e[:1] for d, e in deal.items()}


def _plan(T, topo):
    ranks = list(T.cores)
    root = ranks[T.root]
    world = range((1 + max(topo.host(c) for c in ranks)) * topo.CORES_PER_HOST)
    dies = [topo.die(root)] + sorted(set(topo.die(c) for c in world if _same_chip(topo, c, root)) - {topo.die(root)})

    def rack(c):
        return topo.rack(topo.host(c))

    def spare(chip_of):
        return [c for c in world if _same_chip(topo, c, chip_of) and c not in ranks and topo.may_write(root, c)]

    def pick(chip_of, t, dests, used):
        ok = [c for c in spare(chip_of) if topo.die(c) == dies[t] and c not in used and all(topo.may_write(c, d) for d in dests)]
        return min(ok, key=lambda c: sum(topo.may_write(c, d) for d in ranks))

    bases = [root] + [d for d in ranks if d != root and topo.may_write(root, d) and rack(d) == rack(root)]
    served = dict((b, []) for b in bases)
    for d in ranks:
        if d != root:
            ok = [b for b in bases if any(topo.may_write(c, d) for c in spare(b))]
            served[min(ok, key=lambda b: _links(topo, b, d))].append(d)
    groups = []
    for b in bases:
        far = sorted((d for d in served[b] if rack(d) != rack(b)), key=lambda d: _links(topo, b, d))
        own = [d for d in served[b] if _same_chip(topo, d, b)]
        rest = [d for d in served[b] if d not in far and d not in own]
        gs = [[d] for d in far] + [rest[i:i + PER] for i in range(0, len(rest), PER)]
        gs[0] = gs[0] + own
        groups += [(b, ds) for ds in gs]

    relays, waves = {}, [[], []]
    for t in range(KT):
        for b, dests in groups:
            r = pick(b, t, [d for d in dests if not _same_chip(topo, d, b)], relays)
            relays[r] = (t, dests)
            first = not _same_chip(topo, r, root) or any(rack(d) != rack(r) for d in dests)
            waves[0 if first else 1].append(r)
    return root, relays, [w for w in waves if w]


def _send(g, T, topo, core, deal, pieces, sem_name):
    trs, n = [], 0
    for d, src, dst in pieces:
        rid, pid = topo.addr(d, core)
        trs.append(RemoteDMATransfer(dst_ids=[DstId(rid=rid, pnc=pid)], dma_engine_mask=_mask(deal[d]),
                                     remote_sem=T.sem[sem_name], src=src, dst=dst))
        n += len(deal[d])
    g.remote_dma_fused(trs, local_sem=T.sem.sent)
    return n


def _plane_d(T, t):
    return T["sd%d" % t][:]


def _codes_d(T, t, k):
    return T["wd%d_%d" % (t, k)][:].bitcast(dt.uint8)


def _load_x(T, queues):
    for t in range(KT):
        queues[t].dma_start(T.xb[:, 4 * t * XCOL:4 * (t + 1) * XCOL], T.x[:, 4 * t * XCOL:4 * (t + 1) * XCOL]).then_inc(
            T.sem["lx%d" % t], 16)


def rank_program(g, core, T, topo):
    root, relays, waves = _plan(T, topo)
    sem = T.sem
    fed_p = _first(_deal(topo, root, [r for w in waves for r in w]))
    fed_c = [_deal(topo, root, w) for w in waves]

    if core in relays:
        t, dests = relays[core]
        fed = [f for f in fed_c if core in f][0]
        deal = _deal(topo, core, dests)
        g.wait_ge(sem.s_in, len(fed_p[core]))
        n = _send(g, T, topo, core, deal, [(d, _plane_d(T, t), _plane_d(T, t)) for d in dests], "p%d" % t)
        for k in range(NCH):
            a = t * WCOL + k * CCOL
            g.wait_ge(sem["ci%d" % k], len(fed[core]))
            n += _send(g, T, topo, core, deal, [(d, _codes_d(T, t, k), T.wq[:, a:a + CCOL].bitcast(dt.uint8)) for d in dests],
                       "w%d" % t)
        g.wait_ge(sem.sent, n)
        return

    if T.rank_of(core) is None:
        return

    queues = [g.sync, g.scalar]
    if core == root:
        for t in range(KT):
            queues[t].dma_start(_plane_d(T, t), T.ws[:, t * WCOL:(t + 1) * WCOL]).then_inc(sem.ld_s, 16)
        for k in range(NCH):
            for t in range(KT):
                a = 4 * (t * WCOL + k * CCOL)
                queues[t].dma_start(_codes_d(T, t, k), T.wc[:, a:a + 4 * CCOL]).then_inc(sem["lc%d" % k], 16)
        _load_x(T, queues)
        g.sync.dma_start(T.wq[:].bitcast(dt.uint8), T.wc[:, :]).then_inc(sem.w0, 16)
        g.scalar.dma_start(T.sq[:], T.ws[:, :]).then_inc(sem.w0, 16)
        g.wait_ge(sem.ld_s, 16 * KT)
        n = _send(g, T, topo, core, fed_p, [(r, _plane_d(T, relays[r][0]), _plane_d(T, relays[r][0])) for r in fed_p], "s_in")
        for k in range(NCH):
            g.wait_ge(sem["lc%d" % k], 16 * KT)
            for w, f in zip(waves, fed_c):
                n += _send(g, T, topo, core, f, [(r, _codes_d(T, relays[r][0], k), _codes_d(T, relays[r][0], k)) for r in w],
                           "ci%d" % k)
    else:
        lanes = [0] * KT
        for r, (t, dests) in relays.items():
            if core in dests:
                lanes[t] = len(_deal(topo, r, dests)[core])
        _load_x(T, queues)
        for t in range(KT):
            queues[t].wait_ge(sem["p%d" % t], lanes[t])
            queues[t].dma_start(T.sq[:, t * WCOL:(t + 1) * WCOL], _plane_d(T, t)).then_inc(sem["q%d" % t], 16)

    for t in range(KT):
        g.vector.wait_ge(sem["lx%d" % t], 16)
        g.vector.quantize_mx(T.xq[:, t * XCOL:(t + 1) * XCOL], T.xs[:, t * XCOL:(t + 1) * XCOL],
                             T.xb[:, 4 * t * XCOL:4 * (t + 1) * XCOL]).then_inc(sem["xq%d" % t], 1)
    for h in range(2):
        for t in range(KT):
            if h == 0:
                if core == root:
                    if t == 0:
                        g.tensor.wait_ge(sem.w0, 32)
                else:
                    g.tensor.wait_ge(sem["q%d" % t], 16)
                    g.tensor.wait_ge(sem["w%d" % t], NCH * lanes[t])
                g.tensor.wait_ge(sem["xq%d" % t], 1)
            c = t * XCOL + h * HCOL
            mm = g.tensor.matmul_mx(T.ps[:, 512 * h:512 * h + HCOL], T.wq[:, t * WCOL:(t + 1) * WCOL],
                                    T.sq[:, t * WCOL:(t + 1) * WCOL], T.xq[:, c:c + HCOL], T.xs[:, c:c + HCOL], t == 0, t == KT - 1)
        mm.then_inc(sem["mm%d" % h], 1)
    for h in range(2):
        g.vector.wait_ge(sem["mm%d" % h], 1)
        g.vector.tensor_copy(T.yo[:, h * HCOL:(h + 1) * HCOL], T.ps[:, 512 * h:512 * h + HCOL]).then_inc(sem["cp%d" % h], 1)
    for h in range(2):
        queues[h].wait_ge(sem["cp%d" % h], 1)
        queues[h].dma_start(T.y[:, h * HCOL:(h + 1) * HCOL], T.yo[:, h * HCOL:(h + 1) * HCOL]).then_inc(sem["st%d" % h], 16)
        queues[h].wait_ge(sem["st%d" % h], 16)
    if core == root:
        g.wait_ge(sem.sent, n)
